import numpy as np
import ml_dtypes


def mxq(x, axis, fmt="e4m3"):
    dtype, down = {"e4m3": (ml_dtypes.float8_e4m3fn, 7), "e5m2": (ml_dtypes.float8_e5m2, 14)}[fmt]
    v = np.moveaxis(np.asarray(x, np.float32).astype(ml_dtypes.bfloat16).astype(np.float64), axis, -1)
    blocks = v.reshape(v.shape[:-1] + (-1, 32))
    amax = np.abs(blocks).max(-1, keepdims=True)
    byte = np.maximum(np.where(amax > 0, np.frexp(amax)[1] - 1 + 127, 0) - down, 1)
    scale = np.exp2(byte - 127.0)
    codes = (blocks / scale).astype(np.float32).astype(dtype).astype(np.float64)
    return np.moveaxis((codes * scale).reshape(v.shape), -1, axis)


WIDE = False


def mx_kscale(k):
    if not WIDE:
        return np.ones(k)
    levels = np.array([10, -10, 5, -5, 0])
    if k % 512:
        return np.exp2(np.random.permutation(np.resize(levels, k // 32))).repeat(32)
    a = np.empty((k // 512, 16))
    for p in range(k // 512):
        a[p, :8] = np.random.permutation(np.resize(levels, 8))
        for g in range(8):
            far = levels[np.abs(levels - a[p, g]) >= 10]
            a[p, g + 8] = far[np.random.randint(len(far))]
    return np.exp2(a.ravel()).repeat(32)


def f64(x):
    return np.asarray(x).astype(np.float64)


def striped(idx):
    return np.tile(np.asarray(idx).reshape(-1, 16).T, (8, 1)).astype(np.uint16)


def unstriped(offs):
    return offs[:16].T.reshape(-1).astype(np.int64)


E2M1 = np.array([0.0, 0.5, 1.0, 1.5, 2.0, 3.0, 4.0, 6.0, -0.0, -0.5, -1.0, -1.5, -2.0, -3.0, -4.0, -6.0])


def pack_weight(w, fmt):
    k, n = w.shape
    w = f64(np.asarray(w, np.float32).astype(ml_dtypes.bfloat16)).reshape(k // 32, 32, n)
    amax = np.abs(w).max(1)
    if fmt == "e4m3":
        byte = np.frexp(amax)[1] - 1 + 127 - 7
    else:
        mant, ex = np.frexp(amax / 6.0)
        byte = np.where(mant > 0.5, ex, ex - 1) + 127
    byte = np.clip(np.where(amax > 0, byte, 1), 1, 254)
    scaled = (w * np.exp2(127.0 - byte)[:, None, :]).reshape(k, n).astype(np.float32)
    by_word = np.ascontiguousarray(scaled.reshape(k // 512, 128, 4, n).transpose(0, 1, 3, 2))
    if fmt == "e4m3":
        words = by_word.astype(ml_dtypes.float8_e4m3fn).view(np.uint8)
    else:
        c = by_word.astype(ml_dtypes.float4_e2m1fn).view(np.uint8) & 0xF
        words = (c[..., 0::2] | (c[..., 1::2] << 4)).reshape(k // 512, 128, 2 * n)
    return np.ascontiguousarray(words), np.ascontiguousarray(byte.astype(np.uint8).reshape(k // 512, 16, n))


def unpack_weight(words, scales, fmt):
    g, _, n = scales.shape
    words = np.ascontiguousarray(words).reshape(g, 128, n, -1)
    if fmt == "e4m3":
        vals = words.view(ml_dtypes.float8_e4m3fn).astype(np.float64)
    else:
        nib = np.empty((g, 128, n, 4), np.uint8)
        nib[..., 0::2] = words & 0xF
        nib[..., 1::2] = words >> 4
        vals = E2M1[nib]
    vals = vals * np.repeat(np.exp2(scales.astype(np.float64) - 127.0), 8, axis=1)[..., None]
    return vals.transpose(0, 1, 3, 2).reshape(g * 512, n)


def sigmoid(v):
    return 1.0 / (1.0 + np.exp(-v))


def sgn(shape):
    return np.random.uniform(0.5, 2.0, shape) * np.where(np.random.standard_normal(shape) < 0, -1.0, 1.0)


K, T, J, Q, R, O, N, E = 512, 1024, 256, 128, 512, 128, 256, 256


def setup_inputs():
    n = np.random.standard_normal
    idx = np.random.permutation(T)[:J]
    idx2 = np.random.permutation(J)[:O]
    idx3 = np.random.permutation(E)[:O]
    fk = mx_kscale(K)
    fr = mx_kscale(R)
    fr = fr / fr.max()
    xtp = pack_weight(n((K, T)) / fk[:, None], "e2m1")
    wp = pack_weight(n((K, Q)) * 1 / np.sqrt(K) * fk[:, None], "e4m3")
    wbp = pack_weight(n((R, N)) * 1 / np.sqrt(R) / fr[:, None], "e4m3")
    return {
        "xt_words": xtp[0],
        "xt_scales": xtp[1],
        "w_words": wp[0],
        "w_scales": wp[1],
        "sg": (0.3 * sgn((Q, 1))).astype(np.float32),
        "ba": (np.random.uniform(-3.2, -2.6, (Q, 1)) + np.log(fr[::4])[:, None]).astype(np.float32),
        "bb": (np.random.uniform(-2.5, -2.0, (Q, 1)) + np.log(fr[::4])[:, None]).astype(np.float32),
        "bc": (np.random.uniform(-1.9, -1.4, (Q, 1)) + np.log(fr[::4])[:, None]).astype(np.float32),
        "bd": (np.random.uniform(-1.3, -0.8, (Q, 1)) + np.log(fr[::4])[:, None]).astype(np.float32),
        "wb_words": wbp[0],
        "wb_scales": wbp[1],
        "so": (np.random.uniform(0.5, 1.6, (N, 1))).astype(np.float32),
        "offs": striped(idx),
        "offs2": striped(idx2),
        "offs3": striped(idx3),
    }


def reference(xt_words, xt_scales, w_words, w_scales, sg, ba, bb, bc, bd, wb_words, wb_scales, so, offs, offs2, offs3):
    idx = unstriped(offs)
    idx2 = unstriped(offs2)
    idx3 = unstriped(offs3)
    xtu = unpack_weight(xt_words, xt_scales, "e2m1")
    wu = unpack_weight(w_words, w_scales, "e4m3")
    wbu = unpack_weight(wb_words, wb_scales, "e4m3")
    xtidxg = xtu[:, idx]
    a = wu.T @ xtidxg
    v0 = sigmoid(a[:, idx2] * f64(sg) + f64(ba))
    v1 = sigmoid(a[:, idx2] * f64(sg) + f64(bb))
    v2 = sigmoid(a[:, idx2] * f64(sg) + f64(bc))
    v3 = sigmoid(a[:, idx2] * f64(sg) + f64(bd))
    hid = np.stack([v0, v1, v2, v3], axis=1).reshape(R, O)
    hidq = mxq(hid, 0, "e4m3")
    p = wbu.T @ hidq
    y = np.zeros((N, E))
    y[:, idx3] = p * f64(so)
    return y

@@ -1,0 +1,156 @@
+from contextlib import ExitStack
+
+import concourse.mybir as mybir
+
+F32 = mybir.dt.float32
+BF16 = mybir.dt.bfloat16
+I32 = mybir.dt.int32
+U32 = mybir.dt.uint32
+U16 = mybir.dt.uint16
+U8 = mybir.dt.uint8
+FP8X4 = mybir.dt.float8_e4m3fn_x4
+FP4X4 = mybir.dt.float4_e2m1fn_x4
+ACT = mybir.ActivationFunctionType
+
+K, T, J, Q, R, O, N, E = 512, 1024, 256, 128, 512, 128, 256, 256
+P = 128
+FLOPS = 2 * K * Q * J + 2 * R * N * O
+
+
+def tile_list_thermometer_kernel(
+    tc, xt_words, xt_scales, w_words, w_scales, sg, ba, bb, bc, bd, wb_words, wb_scales, so, offs, offs2, offs3, out
+):
+    nc = tc.nc
+    with ExitStack() as ctx:
+        sb = ctx.enter_context(tc.tile_pool(name="sb", bufs=1))
+        ps = ctx.enter_context(tc.psum_pool(name="ps", bufs=1))
+
+        def tile(name, shape, dtype):
+            return sb.tile(shape, dtype, name=name, align_bytes=64)
+
+        xw = tile("xw", [P, T], U16)
+        xs = tile("xs", [P, T], U8)
+        ww = tile("ww", [P, Q], U32)
+        ws = tile("ws", [P, Q], U8)
+        ws_in = tile("ws_in", [4, 4, Q // 4], I32)
+        wbw = tile("wbw", [P, N], U32)
+        wbs = tile("wbs", [P, N], U8)
+        wbs_in = tile("wbs_in", [4, 4, N // 4], I32)
+        l1 = tile("l1", [P, J // 16], U16)
+        l2 = tile("l2", [P, O // 16], U16)
+        l3 = tile("l3", [P, O // 16], U16)
+        slope = tile("slope", [P, 1], F32)
+        bias = [tile("bias%d" % i, [P, 1], F32) for i in range(4)]
+        gain = tile("gain", [P, 2], F32)
+        pages = [tile("page%d" % t, [P, E], F32) for t in range(2)]
+
+        nc.vector.memset(xs[:].bitcast(I32), 0)
+        nc.vector.memset(ws[:].bitcast(I32), 0)
+        nc.vector.memset(wbs[:].bitcast(I32), 0)
+        for page in pages:
+            nc.vector.memset(page[:], 0.0)
+
+        def rows_by_quadrant(scales):
+            return scales[0].bitcast(I32).rearrange("(q r) c -> r q c", r=4)
+
+        nc.scalar.dma_start(out=ws_in[:], in_=rows_by_quadrant(w_scales))
+        nc.sync.dma_start(l1[:], offs)
+        nc.sync.dma_start(out=xw[:].bitcast(I32), in_=xt_words[0].bitcast(I32))
+        nc.sync.dma_start(
+            out=ww[:].bitcast(I32), in_=w_words[0].rearrange("p c t -> p (c t)").bitcast(I32)
+        )
+        for q in range(4):
+            queue = nc.sync if q < 2 else nc.scalar
+            queue.dma_start(
+                out=xs[32 * q : 32 * q + 4, :].bitcast(I32), in_=xt_scales[0, 4 * q : 4 * q + 4, :].bitcast(I32)
+            )
+        nc.gpsimd.dma_start(out=bias[2][:], in_=bc)
+        nc.gpsimd.dma_start(out=bias[3][:], in_=bd)
+        nc.sync.dma_start(out=slope[:], in_=sg)
+        nc.sync.dma_start(out=bias[0][:], in_=ba)
+        nc.sync.dma_start(l2[:], offs2)
+        nc.sync.dma_start(out=bias[1][:], in_=bb)
+        nc.sync.dma_start(out=wbs_in[:], in_=rows_by_quadrant(wb_scales))
+        nc.sync.dma_start(
+            out=wbw[:].bitcast(I32), in_=wb_words[0].rearrange("p c t -> p (c t)").bitcast(I32)
+        )
+        nc.sync.dma_start(l3[:], offs3)
+        with nc.allow_non_contiguous_dma(reason="one value a partition"):
+            nc.sync.dma_start(out=gain[:], in_=so.rearrange("(t p) o -> p (t o)", p=P))
+
+        def spread(plane, staged):
+            for q in range(4):
+                nc.vector.tensor_copy(out=plane[32 * q : 32 * q + 4, :].bitcast(I32), in_=staged[:, q, :])
+
+        warm_in = tile("warm_in", [P, 1], F32)
+        warm_out = tile("warm_out", [P, 1], F32)
+        nc.vector.memset(warm_in[:], 0.0)
+        nc.scalar.activation(out=warm_out[:], in_=warm_in[:], func=ACT.Sigmoid)
+
+        spread(ws, ws_in)
+
+        gs = tile("gs", [P, J], U8)
+        nc.vector.tensor_copy(out=gs[:], in_=xs[:].indirect(l1[:]))
+        a_sb = tile("a_sb", [P, J], F32)
+        half = J // 2
+        a_ps = []
+        for h in range(2):
+            gw = tile("gw%d" % h, [P, half], U16)
+            nc.vector.tensor_copy(out=gw[:], in_=xw[:].indirect(l1[:, 8 * h : 8 * h + 8]))
+            acc = ps.tile([P, half], F32, name="a_ps%d" % h)
+            nc.tensor.matmul_mx(
+                out=acc[:],
+                lhsT=ww[:].bitcast(FP8X4),
+                lhsT_scale=ws[:],
+                rhs=gw[:].bitcast(FP4X4),
+                rhs_scale=gs[:, h * half : (h + 1) * half],
+                start=True,
+                stop=True,
+            )
+            a_ps.append(acc)
+        for h in range(2):
+            nc.vector.tensor_copy(out=a_sb[:, h * half : (h + 1) * half], in_=a_ps[h][:])
+
+        spread(wbs, wbs_in)
+
+        hid = tile("hid", [P, 4 * O], BF16)
+        codes = tile("codes", [P, O], U32)
+        hs = tile("hs", [P, O], U8)
+        oh = O // 2
+        p_sb = {}
+        for h in range(2):
+            cols = slice(h * oh, (h + 1) * oh)
+            for i in range(4):
+                nc.scalar.activation(
+                    out=hid[:, 4 * h * oh + i : 4 * (h + 1) * oh : 4],
+                    in_=a_sb[:].indirect(l2[:, 4 * h : 4 * h + 4]),
+                    func=ACT.Sigmoid,
+                    bias=bias[i][:],
+                    scale=slope[:],
+                )
+            nc.vector.quantize_mx(
+                out=codes[:, cols].bitcast(FP8X4), scales=hs[:, cols], in_=hid[:, 4 * h * oh : 4 * (h + 1) * oh]
+            )
+            for t in range(2):
+                acc = ps.tile([P, oh], F32, name="p_ps%d%d" % (h, t))
+                nc.tensor.matmul_mx(
+                    out=acc[:],
+                    lhsT=wbw[:, t * P : (t + 1) * P].bitcast(FP8X4),
+                    lhsT_scale=wbs[:, t * P : (t + 1) * P],
+                    rhs=codes[:, cols].bitcast(FP8X4),
+                    rhs_scale=hs[:, cols],
+                    start=True,
+                    stop=True,
+                )
+                p_sb[h, t] = tile("p_sb%d%d" % (h, t), [P, oh], F32)
+                nc.vector.tensor_copy(out=p_sb[h, t][:], in_=acc[:])
+        for h in range(2):
+            for t in range(2):
+                nc.scalar.activation(
+                    out=pages[t][:].indirect(l3[:, 4 * h : 4 * h + 4]),
+                    in_=p_sb[h, t][:],
+                    func=ACT.Copy,
+                    scale=gain[:, t : t + 1],
+                )
+        for t in range(2):
+            nc.sync.dma_start(out=out[t * P : (t + 1) * P, :], in_=pages[t][:])

@@ -82,11 +82,6 @@ def tile_list_thermometer_kernel(
             for q in range(4):
                 nc.vector.tensor_copy(out=plane[32 * q : 32 * q + 4, :].bitcast(I32), in_=staged[:, q, :])
 
-        warm_in = tile("warm_in", [P, 1], F32)
-        warm_out = tile("warm_out", [P, 1], F32)
-        nc.vector.memset(warm_in[:], 0.0)
-        nc.scalar.activation(out=warm_out[:], in_=warm_in[:], func=ACT.Sigmoid)
-
         spread(ws, ws_in)
 
         gs = tile("gs", [P, J], U8)

@@ -25,17 +25,16 @@ def tile_list_thermometer_kernel(
         sb = ctx.enter_context(tc.tile_pool(name="sb", bufs=1))
         ps = ctx.enter_context(tc.psum_pool(name="ps", bufs=1))
 
-        def tile(name, shape, dtype):
-            return sb.tile(shape, dtype, name=name, align_bytes=64)
+        def tile(name, shape, dtype, tag=None):
+            return sb.tile(shape, dtype, name=name, tag=tag or name, align_bytes=64)
 
         xw = tile("xw", [P, T], U16)
         xs = tile("xs", [P, T], U8)
         ww = tile("ww", [P, Q], U32)
-        ws = tile("ws", [P, Q], U8)
+        ws = tile("ws", [P, Q], U8, "weight_plane")
         ws_in = tile("ws_in", [4, 4, Q // 4], I32)
         wbw = tile("wbw", [P, N], U32)
-        wbs = tile("wbs", [P, N], U8)
-        wbs_in = tile("wbs_in", [4, 4, N // 4], I32)
+        wbs_in = tile("wbs_in", [4, 4, N // 4], I32, "staged_then_codes")
         l1 = tile("l1", [P, J // 16], U16)
         l2 = tile("l2", [P, O // 16], U16)
         l3 = tile("l3", [P, O // 16], U16)
@@ -46,7 +45,6 @@ def tile_list_thermometer_kernel(
 
         nc.vector.memset(xs[:].bitcast(I32), 0)
         nc.vector.memset(ws[:].bitcast(I32), 0)
-        nc.vector.memset(wbs[:].bitcast(I32), 0)
         for page in pages:
             nc.vector.memset(page[:], 0.0)
 
@@ -64,19 +62,18 @@ def tile_list_thermometer_kernel(
             queue.dma_start(
                 out=xs[32 * q : 32 * q + 4, :].bitcast(I32), in_=xt_scales[0, 4 * q : 4 * q + 4, :].bitcast(I32)
             )
-        nc.gpsimd.dma_start(out=bias[2][:], in_=bc)
-        nc.gpsimd.dma_start(out=bias[3][:], in_=bd)
+        nc.gpsimd.dma_start(out=wbs_in[:], in_=rows_by_quadrant(wb_scales))
+        with nc.allow_non_contiguous_dma(reason="one value a partition"):
+            nc.gpsimd.dma_start(out=gain[:], in_=so.rearrange("(t p) o -> p (t o)", p=P))
         nc.sync.dma_start(out=slope[:], in_=sg)
         nc.sync.dma_start(out=bias[0][:], in_=ba)
         nc.sync.dma_start(l2[:], offs2)
-        nc.sync.dma_start(out=bias[1][:], in_=bb)
-        nc.sync.dma_start(out=wbs_in[:], in_=rows_by_quadrant(wb_scales))
+        for b_tile, b_in in zip(bias[1:], (bb, bc, bd)):
+            nc.sync.dma_start(out=b_tile[:], in_=b_in)
         nc.sync.dma_start(
             out=wbw[:].bitcast(I32), in_=wb_words[0].rearrange("p c t -> p (c t)").bitcast(I32)
         )
         nc.sync.dma_start(l3[:], offs3)
-        with nc.allow_non_contiguous_dma(reason="one value a partition"):
-            nc.sync.dma_start(out=gain[:], in_=so.rearrange("(t p) o -> p (t o)", p=P))
 
         def spread(plane, staged):
             for q in range(4):
@@ -84,21 +81,21 @@ def tile_list_thermometer_kernel(
 
         spread(ws, ws_in)
 
-        gs = tile("gs", [P, J], U8)
-        nc.vector.tensor_copy(out=gs[:], in_=xs[:].indirect(l1[:]))
+        gw = tile("gw", [P, J], U16)
+        nc.vector.tensor_copy(out=gw[:], in_=xw[:].indirect(l1[:]))
         a_sb = tile("a_sb", [P, J], F32)
         half = J // 2
         a_ps = []
         for h in range(2):
-            gw = tile("gw%d" % h, [P, half], U16)
-            nc.vector.tensor_copy(out=gw[:], in_=xw[:].indirect(l1[:, 8 * h : 8 * h + 8]))
+            gs = tile("gs%d" % h, [P, half], U8)
+            nc.vector.tensor_copy(out=gs[:], in_=xs[:].indirect(l1[:, 8 * h : 8 * h + 8]))
             acc = ps.tile([P, half], F32, name="a_ps%d" % h)
             nc.tensor.matmul_mx(
                 out=acc[:],
                 lhsT=ww[:].bitcast(FP8X4),
                 lhsT_scale=ws[:],
-                rhs=gw[:].bitcast(FP4X4),
-                rhs_scale=gs[:, h * half : (h + 1) * half],
+                rhs=gw[:, h * half : (h + 1) * half].bitcast(FP4X4),
+                rhs_scale=gs[:],
                 start=True,
                 stop=True,
             )
@@ -106,15 +103,14 @@ def tile_list_thermometer_kernel(
         for h in range(2):
             nc.vector.tensor_copy(out=a_sb[:, h * half : (h + 1) * half], in_=a_ps[h][:])
 
+        wbs = tile("wbs", [P, N], U8, "weight_plane")
+        nc.vector.memset(wbs[:].bitcast(I32), 0)
         spread(wbs, wbs_in)
 
         hid = tile("hid", [P, 4 * O], BF16)
-        codes = tile("codes", [P, O], U32)
-        hs = tile("hs", [P, O], U8)
         oh = O // 2
         p_sb = {}
         for h in range(2):
-            cols = slice(h * oh, (h + 1) * oh)
             for i in range(4):
                 nc.scalar.activation(
                     out=hid[:, 4 * h * oh + i : 4 * (h + 1) * oh : 4],
@@ -123,27 +119,29 @@ def tile_list_thermometer_kernel(
                     bias=bias[i][:],
                     scale=slope[:],
                 )
+            codes = tile("codes%d" % h, [P, oh], U32, "staged_then_codes")
+            hs = tile("hs%d" % h, [P, oh], U8)
             nc.vector.quantize_mx(
-                out=codes[:, cols].bitcast(FP8X4), scales=hs[:, cols], in_=hid[:, 4 * h * oh : 4 * (h + 1) * oh]
+                out=codes[:].bitcast(FP8X4), scales=hs[:], in_=hid[:, 4 * h * oh : 4 * (h + 1) * oh]
             )
+            acc = ps.tile([P, 2, oh], F32, name="p_ps%d" % h)
             for t in range(2):
-                acc = ps.tile([P, oh], F32, name="p_ps%d%d" % (h, t))
                 nc.tensor.matmul_mx(
-                    out=acc[:],
+                    out=acc[:, t, :],
                     lhsT=wbw[:, t * P : (t + 1) * P].bitcast(FP8X4),
                     lhsT_scale=wbs[:, t * P : (t + 1) * P],
-                    rhs=codes[:, cols].bitcast(FP8X4),
-                    rhs_scale=hs[:, cols],
+                    rhs=codes[:].bitcast(FP8X4),
+                    rhs_scale=hs[:],
                     start=True,
                     stop=True,
                 )
-                p_sb[h, t] = tile("p_sb%d%d" % (h, t), [P, oh], F32)
-                nc.vector.tensor_copy(out=p_sb[h, t][:], in_=acc[:])
+            p_sb[h] = tile("p_sb%d" % h, [P, 2, oh], F32)
+            nc.vector.tensor_copy(out=p_sb[h][:], in_=acc[:])
         for h in range(2):
             for t in range(2):
                 nc.scalar.activation(
                     out=pages[t][:].indirect(l3[:, 4 * h : 4 * h + 4]),
-                    in_=p_sb[h, t][:],
+                    in_=p_sb[h][:, t, :],
                     func=ACT.Copy,
                     scale=gain[:, t : t + 1],
                 )

@@ -32,7 +32,7 @@ def tile_list_thermometer_kernel(
         xs = tile("xs", [P, T], U8)
         ww = tile("ww", [P, Q], U32)
         ws = tile("ws", [P, Q], U8, "weight_plane")
-        ws_in = tile("ws_in", [4, 4, Q // 4], I32)
+        ws_in = tile("ws_in", [4, 4, Q // 4], I32, "staged_then_warm")
         wbw = tile("wbw", [P, N], U32)
         wbs_in = tile("wbs_in", [4, 4, N // 4], I32, "staged_then_codes")
         l1 = tile("l1", [P, J // 16], U16)
@@ -62,24 +62,30 @@ def tile_list_thermometer_kernel(
             queue.dma_start(
                 out=xs[32 * q : 32 * q + 4, :].bitcast(I32), in_=xt_scales[0, 4 * q : 4 * q + 4, :].bitcast(I32)
             )
-        nc.gpsimd.dma_start(out=wbs_in[:], in_=rows_by_quadrant(wb_scales))
-        with nc.allow_non_contiguous_dma(reason="one value a partition"):
-            nc.gpsimd.dma_start(out=gain[:], in_=so.rearrange("(t p) o -> p (t o)", p=P))
+        nc.gpsimd.dma_start(out=bias[3][:], in_=bd)
         nc.sync.dma_start(out=slope[:], in_=sg)
         nc.sync.dma_start(out=bias[0][:], in_=ba)
         nc.sync.dma_start(l2[:], offs2)
-        for b_tile, b_in in zip(bias[1:], (bb, bc, bd)):
+        for b_tile, b_in in zip(bias[1:3], (bb, bc)):
             nc.sync.dma_start(out=b_tile[:], in_=b_in)
+        nc.sync.dma_start(out=wbs_in[:], in_=rows_by_quadrant(wb_scales))
         nc.sync.dma_start(
             out=wbw[:].bitcast(I32), in_=wb_words[0].rearrange("p c t -> p (c t)").bitcast(I32)
         )
         nc.sync.dma_start(l3[:], offs3)
+        with nc.allow_non_contiguous_dma(reason="one value a partition"):
+            nc.sync.dma_start(out=gain[:], in_=so.rearrange("(t p) o -> p (t o)", p=P))
 
         def spread(plane, staged):
             for q in range(4):
                 nc.vector.tensor_copy(out=plane[32 * q : 32 * q + 4, :].bitcast(I32), in_=staged[:, q, :])
 
         spread(ws, ws_in)
+
+        warm_in = tile("warm_in", [P, 1], F32, "staged_then_warm")
+        warm_out = tile("warm_out", [P, 1], F32)
+        nc.vector.memset(warm_in[:], 0.0)
+        nc.scalar.activation(out=warm_out[:], in_=warm_in[:], func=ACT.Sigmoid)
 
         gw = tile("gw", [P, J], U16)
         nc.vector.tensor_copy(out=gw[:], in_=xw[:].indirect(l1[:]))
@@ -107,27 +113,27 @@ def tile_list_thermometer_kernel(
         nc.vector.memset(wbs[:].bitcast(I32), 0)
         spread(wbs, wbs_in)
 
-        hid = tile("hid", [P, 4 * O], BF16)
         oh = O // 2
         p_sb = {}
         for h in range(2):
+            hid = tile("hid%d" % h, [P, 4 * oh], BF16)
             for i in range(4):
                 nc.scalar.activation(
-                    out=hid[:, 4 * h * oh + i : 4 * (h + 1) * oh : 4],
+                    out=hid[:, i : 4 * oh : 4],
                     in_=a_sb[:].indirect(l2[:, 4 * h : 4 * h + 4]),
                     func=ACT.Sigmoid,
                     bias=bias[i][:],
                     scale=slope[:],
                 )
-            codes = tile("codes%d" % h, [P, oh], U32, "staged_then_codes")
+            codes = tile("codes%d" % h, [P, oh], U32, "staged_then_codes" if h == 0 else None)
             hs = tile("hs%d" % h, [P, oh], U8)
             nc.vector.quantize_mx(
-                out=codes[:].bitcast(FP8X4), scales=hs[:], in_=hid[:, 4 * h * oh : 4 * (h + 1) * oh]
+                out=codes[:].bitcast(FP8X4), scales=hs[:], in_=hid[:]
             )
-            acc = ps.tile([P, 2, oh], F32, name="p_ps%d" % h)
             for t in range(2):
+                acc = ps.tile([P, oh], F32, name="p_ps%d%d" % (h, t))
                 nc.tensor.matmul_mx(
-                    out=acc[:, t, :],
+                    out=acc[:],
                     lhsT=wbw[:, t * P : (t + 1) * P].bitcast(FP8X4),
                     lhsT_scale=wbs[:, t * P : (t + 1) * P],
                     rhs=codes[:].bitcast(FP8X4),
@@ -135,13 +141,13 @@ def tile_list_thermometer_kernel(
                     start=True,
                     stop=True,
                 )
-            p_sb[h] = tile("p_sb%d" % h, [P, 2, oh], F32)
-            nc.vector.tensor_copy(out=p_sb[h][:], in_=acc[:])
+                p_sb[h, t] = tile("p_sb%d%d" % (h, t), [P, oh], F32)
+                nc.vector.tensor_copy(out=p_sb[h, t][:], in_=acc[:])
         for h in range(2):
             for t in range(2):
                 nc.scalar.activation(
                     out=pages[t][:].indirect(l3[:, 4 * h : 4 * h + 4]),
-                    in_=p_sb[h][:, t, :],
+                    in_=p_sb[h, t][:],
                     func=ACT.Copy,
                     scale=gain[:, t : t + 1],
                 )

@@ -32,7 +32,7 @@ def tile_list_thermometer_kernel(
         xs = tile("xs", [P, T], U8)
         ww = tile("ww", [P, Q], U32)
         ws = tile("ws", [P, Q], U8, "weight_plane")
-        ws_in = tile("ws_in", [4, 4, Q // 4], I32, "staged_then_warm")
+        ws_in = tile("ws_in", [4, 4, Q // 4], I32)
         wbw = tile("wbw", [P, N], U32)
         wbs_in = tile("wbs_in", [4, 4, N // 4], I32, "staged_then_codes")
         l1 = tile("l1", [P, J // 16], U16)
@@ -81,11 +81,6 @@ def tile_list_thermometer_kernel(
                 nc.vector.tensor_copy(out=plane[32 * q : 32 * q + 4, :].bitcast(I32), in_=staged[:, q, :])
 
         spread(ws, ws_in)
-
-        warm_in = tile("warm_in", [P, 1], F32, "staged_then_warm")
-        warm_out = tile("warm_out", [P, 1], F32)
-        nc.vector.memset(warm_in[:], 0.0)
-        nc.scalar.activation(out=warm_out[:], in_=warm_in[:], func=ACT.Sigmoid)
 
         gw = tile("gw", [P, J], U16)
         nc.vector.tensor_copy(out=gw[:], in_=xw[:].indirect(l1[:]))

from contextlib import ExitStack

import concourse.mybir as mybir

F32 = mybir.dt.float32
BF16 = mybir.dt.bfloat16
I32 = mybir.dt.int32
U32 = mybir.dt.uint32
U16 = mybir.dt.uint16
U8 = mybir.dt.uint8
FP8X4 = mybir.dt.float8_e4m3fn_x4
FP4X4 = mybir.dt.float4_e2m1fn_x4
ACT = mybir.ActivationFunctionType

K, T, J, Q, R, O, N, E = 512, 1024, 256, 128, 512, 128, 256, 256
P = 128
FLOPS = 2 * K * Q * J + 2 * R * N * O


def tile_list_thermometer_kernel(
    tc, xt_words, xt_scales, w_words, w_scales, sg, ba, bb, bc, bd, wb_words, wb_scales, so, offs, offs2, offs3, out
):
    nc = tc.nc
    with ExitStack() as ctx:
        sb = ctx.enter_context(tc.tile_pool(name="sb", bufs=1))
        ps = ctx.enter_context(tc.psum_pool(name="ps", bufs=1))

        def tile(name, shape, dtype, tag=None):
            return sb.tile(shape, dtype, name=name, tag=tag or name, align_bytes=64)

        xw = tile("xw", [P, T], U16)
        xs = tile("xs", [P, T], U8)
        ww = tile("ww", [P, Q], U32)
        ws = tile("ws", [P, Q], U8, "weight_plane")
        ws_in = tile("ws_in", [4, 4, Q // 4], I32)
        wbw = tile("wbw", [P, N], U32)
        wbs_in = tile("wbs_in", [4, 4, N // 4], I32, "staged_then_codes")
        l1 = tile("l1", [P, J // 16], U16)
        l2 = tile("l2", [P, O // 16], U16)
        l3 = tile("l3", [P, O // 16], U16)
        slope = tile("slope", [P, 1], F32)
        bias = [tile("bias%d" % i, [P, 1], F32) for i in range(4)]
        gain = tile("gain", [P, 2], F32)
        pages = [tile("page%d" % t, [P, E], F32) for t in range(2)]

        nc.vector.memset(xs[:].bitcast(I32), 0)
        nc.vector.memset(ws[:].bitcast(I32), 0)
        for page in pages:
            nc.vector.memset(page[:], 0.0)

        def rows_by_quadrant(scales):
            return scales[0].bitcast(I32).rearrange("(q r) c -> r q c", r=4)

        nc.scalar.dma_start(out=ws_in[:], in_=rows_by_quadrant(w_scales))
        nc.sync.dma_start(l1[:], offs)
        nc.sync.dma_start(out=xw[:].bitcast(I32), in_=xt_words[0].bitcast(I32))
        nc.sync.dma_start(
            out=ww[:].bitcast(I32), in_=w_words[0].rearrange("p c t -> p (c t)").bitcast(I32)
        )
        for q in range(4):
            queue = nc.sync if q < 2 else nc.scalar
            queue.dma_start(
                out=xs[32 * q : 32 * q + 4, :].bitcast(I32), in_=xt_scales[0, 4 * q : 4 * q + 4, :].bitcast(I32)
            )
        nc.gpsimd.dma_start(out=bias[3][:], in_=bd)
        nc.sync.dma_start(out=slope[:], in_=sg)
        nc.sync.dma_start(out=bias[0][:], in_=ba)
        nc.sync.dma_start(l2[:], offs2)
        for b_tile, b_in in zip(bias[1:3], (bb, bc)):
            nc.sync.dma_start(out=b_tile[:], in_=b_in)
        nc.sync.dma_start(out=wbs_in[:], in_=rows_by_quadrant(wb_scales))
        nc.sync.dma_start(
            out=wbw[:].bitcast(I32), in_=wb_words[0].rearrange("p c t -> p (c t)").bitcast(I32)
        )
        nc.sync.dma_start(l3[:], offs3)
        with nc.allow_non_contiguous_dma(reason="one value a partition"):
            nc.sync.dma_start(out=gain[:], in_=so.rearrange("(t p) o -> p (t o)", p=P))

        def spread(plane, staged):
            for q in range(4):
                nc.vector.tensor_copy(out=plane[32 * q : 32 * q + 4, :].bitcast(I32), in_=staged[:, q, :])

        spread(ws, ws_in)

        gw = tile("gw", [P, J], U16)
        nc.vector.tensor_copy(out=gw[:], in_=xw[:].indirect(l1[:]))
        a_sb = tile("a_sb", [P, J], F32)
        half = J // 2
        a_ps = []
        for h in range(2):
            gs = tile("gs%d" % h, [P, half], U8)
            nc.vector.tensor_copy(out=gs[:], in_=xs[:].indirect(l1[:, 8 * h : 8 * h + 8]))
            acc = ps.tile([P, half], F32, name="a_ps%d" % h)
            nc.tensor.matmul_mx(
                out=acc[:],
                lhsT=ww[:].bitcast(FP8X4),
                lhsT_scale=ws[:],
                rhs=gw[:, h * half : (h + 1) * half].bitcast(FP4X4),
                rhs_scale=gs[:],
                start=True,
                stop=True,
            )
            a_ps.append(acc)
        for h in range(2):
            nc.vector.tensor_copy(out=a_sb[:, h * half : (h + 1) * half], in_=a_ps[h][:])

        wbs = tile("wbs", [P, N], U8, "weight_plane")
        nc.vector.memset(wbs[:].bitcast(I32), 0)
        spread(wbs, wbs_in)

        oh = O // 2
        p_sb = {}
        for h in range(2):
            hid = tile("hid%d" % h, [P, 4 * oh], BF16)
            for i in range(4):
                nc.scalar.activation(
                    out=hid[:, i : 4 * oh : 4],
                    in_=a_sb[:].indirect(l2[:, 4 * h : 4 * h + 4]),
                    func=ACT.Sigmoid,
                    bias=bias[i][:],
                    scale=slope[:],
                )
            codes = tile("codes%d" % h, [P, oh], U32, "staged_then_codes" if h == 0 else None)
            hs = tile("hs%d" % h, [P, oh], U8)
            nc.vector.quantize_mx(
                out=codes[:].bitcast(FP8X4), scales=hs[:], in_=hid[:]
            )
            for t in range(2):
                acc = ps.tile([P, oh], F32, name="p_ps%d%d" % (h, t))
                nc.tensor.matmul_mx(
                    out=acc[:],
                    lhsT=wbw[:, t * P : (t + 1) * P].bitcast(FP8X4),
                    lhsT_scale=wbs[:, t * P : (t + 1) * P],
                    rhs=codes[:].bitcast(FP8X4),
                    rhs_scale=hs[:],
                    start=True,
                    stop=True,
                )
                p_sb[h, t] = tile("p_sb%d%d" % (h, t), [P, oh], F32)
                nc.vector.tensor_copy(out=p_sb[h, t][:], in_=acc[:])
        for h in range(2):
            for t in range(2):
                nc.scalar.activation(
                    out=pages[t][:].indirect(l3[:, 4 * h : 4 * h + 4]),
                    in_=p_sb[h, t][:],
                    func=ACT.Copy,
                    scale=gain[:, t : t + 1],
                )
        for t in range(2):
            nc.sync.dma_start(out=out[t * P : (t + 1) * P, :], in_=pages[t][:])
